import numpy as np
import ml_dtypes


def mxq(x, axis, fmt="e4m3"):
    dtype, down = {"e4m3": (ml_dtypes.float8_e4m3fn, 7), "e5m2": (ml_dtypes.float8_e5m2, 14)}[fmt]
    v = np.moveaxis(np.asarray(x, np.float32).astype(ml_dtypes.bfloat16).astype(np.float64), axis, -1)
    blocks = v.reshape(v.shape[:-1] + (-1, 32))
    amax = np.abs(blocks).max(-1, keepdims=True)
    byte = np.maximum(np.where(amax > 0, np.frexp(amax)[1] - 1 + 127, 0) - down, 1)
    scale = np.exp2(byte - 127.0)
    codes = (blocks / scale).astype(np.float32).astype(dtype).astype(np.float64)
    return np.moveaxis((codes * scale).reshape(v.shape), -1, axis)


WIDE = False


def mx_kscale(k):
    if not WIDE:
        return np.ones(k)
    levels = np.array([10, -10, 5, -5, 0])
    if k % 512:
        return np.exp2(np.random.permutation(np.resize(levels, k // 32))).repeat(32)
    a = np.empty((k // 512, 16))
    for p in range(k // 512):
        a[p, :8] = np.random.permutation(np.resize(levels, 8))
        for g in range(8):
            far = levels[np.abs(levels - a[p, g]) >= 10]
            a[p, g + 8] = far[np.random.randint(len(far))]
    return np.exp2(a.ravel()).repeat(32)


def f64(x):
    return np.asarray(x).astype(np.float64)


def striped(idx):
    return np.tile(idx.reshape(-1, 16).T, (8, 1)).astype(np.uint16)


def unstriped(offs):
    return offs[:16].T.reshape(-1).astype(np.int64)


E2M1 = np.array([0.0, 0.5, 1.0, 1.5, 2.0, 3.0, 4.0, 6.0, -0.0, -0.5, -1.0, -1.5, -2.0, -3.0, -4.0, -6.0])


def pack_weight(w, fmt):
    k, n = w.shape
    w = f64(np.asarray(w, np.float32).astype(ml_dtypes.bfloat16)).reshape(k // 32, 32, n)
    amax = np.abs(w).max(1)
    if fmt == "e4m3":
        byte = np.frexp(amax)[1] - 1 + 127 - 7
    else:
        mant, ex = np.frexp(amax / 6.0)
        byte = np.where(mant > 0.5, ex, ex - 1) + 127
    byte = np.clip(np.where(amax > 0, byte, 1), 1, 254)
    scaled = (w * np.exp2(127.0 - byte)[:, None, :]).reshape(k, n).astype(np.float32)
    by_word = np.ascontiguousarray(scaled.reshape(k // 512, 128, 4, n).transpose(0, 1, 3, 2))
    if fmt == "e4m3":
        words = by_word.astype(ml_dtypes.float8_e4m3fn).view(np.uint8)
    else:
        c = by_word.astype(ml_dtypes.float4_e2m1fn).view(np.uint8) & 0xF
        words = (c[..., 0::2] | (c[..., 1::2] << 4)).reshape(k // 512, 128, 2 * n)
    return np.ascontiguousarray(words), np.ascontiguousarray(byte.astype(np.uint8).reshape(k // 512, 16, n))


def unpack_weight(words, scales, fmt):
    g, _, n = scales.shape
    words = np.ascontiguousarray(words).reshape(g, 128, n, -1)
    if fmt == "e4m3":
        vals = words.view(ml_dtypes.float8_e4m3fn).astype(np.float64)
    else:
        nib = np.empty((g, 128, n, 4), np.uint8)
        nib[..., 0::2] = words & 0xF
        nib[..., 1::2] = words >> 4
        vals = E2M1[nib]
    vals = vals * np.repeat(np.exp2(scales.astype(np.float64) - 127.0), 8, axis=1)[..., None]
    return vals.transpose(0, 1, 3, 2).reshape(g * 512, n)


def gelu(v):
    return 0.5 * v * (1.0 + np.tanh(np.sqrt(2.0 / np.pi) * (v + 0.044715 * v**3)))


K, T, S, H, N = 1024, 4096, 512, 1536, 512


def setup_inputs():
    n = np.random.standard_normal
    s = mx_kscale(K)[:, None]
    u = mx_kscale(H)[:, None]
    tab_words, tab_scales = pack_weight(n((K, T)) * s, "e4m3")
    w1 = (n((K, H)) / np.sqrt(K) / s * u.T).astype(np.float32)
    w4_words, w4_scales = pack_weight(n((H, N)) / np.sqrt(H) / u, "e2m1")
    return {
        "tab_words": tab_words,
        "tab_scales": tab_scales,
        "offs": striped(np.random.permutation(T)[:S]),
        "offs2": striped(np.random.permutation(T)[:S]),
        "offs3": striped(np.random.permutation(T)[:S]),
        "w1": w1,
        "w4_words": w4_words,
        "w4_scales": w4_scales,
    }


def reference(tab_words, tab_scales, offs, offs2, offs3, w1, w4_words, w4_scales):
    TW = unpack_weight(tab_words, tab_scales, "e4m3")
    v = TW[:, unstriped(offs)]
    v2 = TW[:, unstriped(offs2)]
    v3 = TW[:, unstriped(offs3)]
    w1q = mxq(f64(w1), 0, "e4m3")
    brand = w1q.T @ v
    factory = w1q.T @ v2
    sub = w1q.T @ v3
    h = np.abs(brand - factory) + np.abs(factory - sub)
    hq = mxq(h, 0, "e4m3")
    w4 = unpack_weight(w4_words, w4_scales, "e2m1")
    return w4.T @ hq

@@ -1,0 +1,253 @@
+from contextlib import ExitStack
+
+import concourse.mybir as mybir
+
+K, T, S, H, N = 1024, 4096, 512, 1536, 512
+FLOPS = 2 * K * H * S * 3 + 2 * H * N * S
+
+F32 = mybir.dt.float32
+BF16 = mybir.dt.bfloat16
+I32 = mybir.dt.int32
+U32 = mybir.dt.uint32
+U16 = mybir.dt.uint16
+U8 = mybir.dt.uint8
+FP8X4 = mybir.dt.float8_e4m3fn_x4
+FP4X4 = mybir.dt.float4_e2m1fn_x4
+ALU = mybir.AluOpType
+ACT = mybir.ActivationFunctionType
+
+P = 128
+PACK = 4
+PASS = P * PACK
+KP = K // PASS
+HP = H // PASS
+JH = 256
+JQ = 128
+BRAND, FACTORY, SUB = 0, 1, 2
+
+
+def tile_list_audit_leakage_scores_kernel(tc, tab_words, tab_scales, offs, offs2, offs3, w1, w4_words, w4_scales, out):
+    nc = tc.nc
+    with ExitStack() as ctx:
+        keep = ctx.enter_context(tc.tile_pool(name="keep", bufs=1))
+        work = ctx.enter_context(tc.tile_pool(name="work", bufs=2))
+        psum = ctx.enter_context(tc.psum_pool(name="psum", bufs=1))
+
+        lists = []
+        for x, src in enumerate((offs, offs2, offs3)):
+            lst = keep.tile([P, S // 16], U16, name=f"list{x}")
+            nc.sync.dma_start(lst[:], src)
+            lists.append(lst)
+
+        tsc = keep.tile([P, T], U8, name="tsc", align_bytes=64)
+        nc.vector.memset(tsc[:].bitcast(I32), 0)
+        for q in range(4):
+            nc.gpsimd.dma_start(tsc[32 * q : 32 * q + 8, :].bitcast(I32), tab_scales[:, 4 * q : 4 * q + 4, :].bitcast(I32))
+
+        tw = []
+        for a in range(KP):
+            t = keep.tile([P, T], U32, name=f"tw{a}", align_bytes=64)
+            nc.sync.dma_start(t[:].bitcast(I32), tab_words[a].rearrange("p t i -> p (t i)").bitcast(I32))
+            tw.append(t)
+
+        raw = {}
+        for b in range(HP):
+            for a in range(KP):
+                r = keep.tile([P, PACK, PASS], F32, name=f"raw{b}{a}", align_bytes=64)
+                nc.sync.dma_start(r[:], w1[a * PASS : (a + 1) * PASS, b * PASS : (b + 1) * PASS].rearrange("(p i) c -> p i c", i=PACK))
+                raw[b, a] = r
+
+        w4c = keep.tile([P, HP, 2 * N], U8, name="w4c", align_bytes=64)
+        nc.sync.dma_start(w4c[:].bitcast(I32), w4_words.rearrange("a p c -> p a c").bitcast(I32))
+        w4s = keep.tile([P, HP, N], U8, name="w4s", align_bytes=64)
+        nc.vector.memset(w4s[:].bitcast(I32), 0)
+        for q in range(4):
+            nc.sync.dma_start(
+                w4s[32 * q : 32 * q + 4, :, :].bitcast(I32),
+                w4_scales[:, 4 * q : 4 * q + 4, :].rearrange("a r c -> r a c").bitcast(I32),
+            )
+
+        order = (FACTORY, BRAND, SUB)
+        gs, gw = {}, {}
+        for x in order:
+            g = keep.tile([P, S], U8, name=f"gs{x}", align_bytes=64)
+            nc.vector.tensor_copy(g[:], tsc[:].indirect(lists[x][:]))
+            gs[x] = g
+        for a in range(KP):
+            for x in order:
+                g = keep.tile([P, S], U32, name=f"gw{x}{a}", align_bytes=64)
+                nc.vector.tensor_copy(g[:], tw[a][:].indirect(lists[x][:]))
+                gw[x, a] = g
+
+        grouped, w1c, w1s = {}, {}, {}
+
+        def cast_w1(b, a, u, on_vector):
+            g = work.tile([P, 2, P, PACK], BF16, name="w1g", bufs=4, align_bytes=64)
+            src = raw[b, a][:].rearrange("p i (m t) -> p m t i", t=PACK)[:, :, 2 * u : 2 * u + 2, :]
+            dst = g[:].rearrange("p e m i -> p m e i")
+            if on_vector:
+                nc.vector.tensor_copy(dst, src)
+            else:
+                nc.scalar.copy(dst, src)
+            grouped[b, a, u] = g
+
+        def quant_w1(b, a, u):
+            c = keep.tile([P, 2 * P], U32, name=f"w1c{b}{a}{u}", align_bytes=64)
+            s = keep.tile([P, 2 * P], U8, name=f"w1s{b}{a}{u}", align_bytes=64)
+            nc.vector.quantize_mx(out=c[:].bitcast(FP8X4), scales=s[:], in_=grouped[b, a, u][:].rearrange("p e m i -> p (e m i)"))
+            w1c[b, a, u], w1s[b, a, u] = c, s
+
+        steps = [(b, jh * JH, JH, (2 * u, 2 * u + 1)) for b in range(HP) for jh in range(2) for u in range(2)][:-2]
+        steps = steps + [(HP - 1, JH + c * JQ, JQ, (0, 1, 2, 3)) for c in range(2)]
+        banks, fs, dif, mag, hb, hc, hs = {}, {}, {}, {}, {}, {}, {}
+
+        def products(k):
+            b, j0, width, ts = steps[k]
+            cols = slice(j0, j0 + width)
+            for x in order:
+                banks[k, x] = psum.tile([P, len(ts), width], F32, name=f"bank{x}", bufs=2)
+            if k == 0:
+                seq = [(x, a) for a in range(KP) for x in order]
+            else:
+                seq = [(x, a) for x in order for a in range(KP)]
+            for x, a in seq:
+                for i, t in enumerate(ts):
+                    u, e = divmod(t, 2)
+                    nc.tensor.matmul_mx(
+                        out=banks[k, x][:, i, :],
+                        lhsT=w1c[b, a, u][:, e * P : (e + 1) * P].bitcast(FP8X4),
+                        lhsT_scale=w1s[b, a, u][:, e * P : (e + 1) * P],
+                        rhs=gw[x, a][:, cols].bitcast(FP8X4),
+                        rhs_scale=gs[x][4 * a : P, cols],
+                        start=(a == 0 and i == 0),
+                        stop=(a == KP - 1 and i == len(ts) - 1),
+                    )
+
+        def copy_factory(k):
+            b, j0, width, ts = steps[k]
+            f = work.tile([P, width, len(ts)], F32, name="fs", bufs=3)
+            nc.scalar.copy(f[:], banks[k, FACTORY][:].rearrange("p e n -> p n e"))
+            fs[k] = f
+
+        def differences(k):
+            b, j0, width, ts = steps[k]
+            for y, x in enumerate((BRAND, SUB)):
+                d = work.tile([P, width, len(ts)], F32, name="dif", bufs=6)
+                nc.vector.tensor_tensor(d[:], banks[k, x][:].rearrange("p e n -> p n e"), fs[k][:], ALU.subtract)
+                dif[k, y] = d
+
+        def magnitudes(k):
+            b, j0, width, ts = steps[k]
+            parts = PACK // len(ts)
+            if ts[0] == 0:
+                for y in range(2):
+                    mag[b, j0, y] = work.tile([P, parts, width, len(ts)], F32, name="mag", bufs=4)
+            for y in range(2):
+                nc.scalar.activation(mag[b, j0, y][:, ts[0] // len(ts)], dif[k, y][:], ACT.Abs)
+
+        def add_h(k):
+            b, j0, width, ts = steps[k]
+            h = work.tile([P, width, PACK // len(ts), len(ts)], BF16, name="hb", bufs=2, align_bytes=64)
+            nc.vector.tensor_tensor(
+                h[:], mag[b, j0, 0][:].rearrange("p u n e -> p n u e"), mag[b, j0, 1][:].rearrange("p u n e -> p n u e"), ALU.add
+            )
+            hb[b, j0] = h
+
+        def quant_h(k):
+            b, j0, width, ts = steps[k]
+            c = keep.tile([P, width], U32, name=f"hc{b}{j0}", align_bytes=64)
+            s = keep.tile([P, width], U8, name=f"hs{b}{j0}", align_bytes=64)
+            nc.vector.quantize_mx(out=c[:].bitcast(FP8X4), scales=s[:], in_=hb[b, j0][:].rearrange("p n u e -> p (n u e)"))
+            hc[b, j0], hs[b, j0] = c, s
+
+        outs = [
+            (0, JH, (0, 1), "obank0", 1),
+            (0, JH, (2, 3), "obank1", 1),
+            (JH, JQ, (0, 1, 2, 3), f"bank{FACTORY}", 2),
+            (JH + JQ, JQ, (0, 1), f"bank{BRAND}", 2),
+            (JH + JQ, JQ, (2, 3), f"bank{SUB}", 2),
+        ]
+        obank = {}
+
+        def scores(o, b):
+            j0, width, ys, tag, depth = outs[o]
+            if b == 0:
+                obank[o] = psum.tile([P, len(ys), width], F32, name=tag, bufs=depth)
+            base = j0 if (b, j0) in hc else JH
+            cols = slice(j0 - base, j0 - base + width)
+            for i, y in enumerate(ys):
+                nc.tensor.matmul_mx(
+                    out=obank[o][:, i, :],
+                    lhsT=w4c[:, b, 2 * y * P : 2 * (y + 1) * P].bitcast(FP4X4),
+                    lhsT_scale=w4s[:, b, y * P : (y + 1) * P],
+                    rhs=hc[b, base][:, cols].bitcast(FP8X4),
+                    rhs_scale=hs[b, base][:, cols],
+                    start=(b == 0 and i == 0),
+                    stop=(b == HP - 1 and i == len(ys) - 1),
+                )
+
+        def store(o, on_vector):
+            j0, width, ys, tag, depth = outs[o]
+            res = work.tile([P, len(ys), width], F32, name="res", bufs=5)
+            if on_vector:
+                nc.vector.tensor_copy(res[:], obank[o][:])
+            else:
+                nc.scalar.copy(res[:], obank[o][:])
+            rows = out[ys[0] * P : (ys[-1] + 1) * P, j0 : j0 + width]
+            nc.sync.dma_start(rows.rearrange("(y p) c -> p y c", p=P), res[:])
+
+        cast_w1(0, 0, 0, False)
+        cast_w1(0, 0, 1, False)
+        quant_w1(0, 0, 0)
+        cast_w1(0, 1, 0, True)
+        cast_w1(0, 1, 1, False)
+        quant_w1(0, 1, 0)
+        quant_w1(0, 0, 1)
+        quant_w1(0, 1, 1)
+
+        ahead = ((0, 0), (1, 0), (0, 1), (1, 1))
+        on_vector = {(1, 1, 0), (1, 1, 1), (2, 1, 0)}
+
+        last = len(steps) - 1
+        products(0)
+        copy_factory(0)
+        products(1)
+        for k in range(len(steps)):
+            b = steps[k][0]
+            if k + 1 <= last:
+                copy_factory(k + 1)
+            differences(k)
+            if k + 2 <= last and steps[k + 2][0] == b:
+                products(k + 2)
+            magnitudes(k)
+            if b + 1 < HP:
+                a2, u2 = ahead[k % 4]
+                cast_w1(b + 1, a2, u2, (b + 1, a2, u2) in on_vector)
+            if k >= 1 and steps[k - 1][3][-1] == PACK - 1:
+                add_h(k - 1)
+            if b + 1 < HP and k % 4 >= 1:
+                quant_w1(b + 1, *ahead[k % 4 - 1])
+            if k >= 2 and steps[k - 2][3][-1] == PACK - 1:
+                quant_h(k - 2)
+                if steps[k - 2][1] == 0:
+                    scores(0, steps[k - 2][0])
+                    scores(1, steps[k - 2][0])
+            if b + 1 < HP and k % 4 == 3:
+                quant_w1(b + 1, 1, 1)
+            if k + 2 <= last and steps[k + 2][0] != b:
+                products(k + 2)
+            if k == last - 1:
+                for o in (2, 3, 4):
+                    scores(o, 0)
+                    scores(o, 1)
+        quant_h(last - 1)
+        add_h(last)
+        scores(2, HP - 1)
+        store(0, False)
+        quant_h(last)
+        scores(3, HP - 1)
+        scores(4, HP - 1)
+        store(1, True)
+        store(2, False)
+        store(3, False)
+        store(4, True)

@@ -30,61 +30,78 @@ def tile_list_audit_leakage_scores_kernel(tc, tab_words, tab_scales, offs, offs2
     nc = tc.nc
     with ExitStack() as ctx:
         keep = ctx.enter_context(tc.tile_pool(name="keep", bufs=1))
+        over = ctx.enter_context(tc.tile_pool(name="over", bufs=1))
         work = ctx.enter_context(tc.tile_pool(name="work", bufs=2))
         psum = ctx.enter_context(tc.psum_pool(name="psum", bufs=1))
 
+        KB = 1024
+        tsc = over.tile([P, T], U8, name="tsc", align_bytes=64, offset=6 * KB)
+        nc.vector.memset(tsc[:].bitcast(I32), 0)
         lists = []
         for x, src in enumerate((offs, offs2, offs3)):
             lst = keep.tile([P, S // 16], U16, name=f"list{x}")
             nc.sync.dma_start(lst[:], src)
             lists.append(lst)
-
-        tsc = keep.tile([P, T], U8, name="tsc", align_bytes=64)
-        nc.vector.memset(tsc[:].bitcast(I32), 0)
-        for q in range(4):
-            nc.gpsimd.dma_start(tsc[32 * q : 32 * q + 8, :].bitcast(I32), tab_scales[:, 4 * q : 4 * q + 4, :].bitcast(I32))
+        nc.sync.dma_start(tsc[0:P:4, :].bitcast(I32), tab_scales.rearrange("a q t -> (a q) t").bitcast(I32))
 
         tw = []
         for a in range(KP):
-            t = keep.tile([P, T], U32, name=f"tw{a}", align_bytes=64)
+            t = over.tile([P, T], U32, name=f"tw{a}", align_bytes=64, offset=16 * KB * (a + 1))
             nc.sync.dma_start(t[:].bitcast(I32), tab_words[a].rearrange("p t i -> p (t i)").bitcast(I32))
             tw.append(t)
 
-        raw = {}
-        for b in range(HP):
-            for a in range(KP):
-                r = keep.tile([P, PACK, PASS], F32, name=f"raw{b}{a}", align_bytes=64)
-                nc.sync.dma_start(r[:], w1[a * PASS : (a + 1) * PASS, b * PASS : (b + 1) * PASS].rearrange("(p i) c -> p i c", i=PACK))
-                raw[b, a] = r
-
-        w4c = keep.tile([P, HP, 2 * N], U8, name="w4c", align_bytes=64)
-        nc.sync.dma_start(w4c[:].bitcast(I32), w4_words.rearrange("a p c -> p a c").bitcast(I32))
-        w4s = keep.tile([P, HP, N], U8, name="w4s", align_bytes=64)
-        nc.vector.memset(w4s[:].bitcast(I32), 0)
-        for q in range(4):
-            nc.sync.dma_start(
-                w4s[32 * q : 32 * q + 4, :, :].bitcast(I32),
-                w4_scales[:, 4 * q : 4 * q + 4, :].rearrange("a r c -> r a c").bitcast(I32),
-            )
-
         order = (FACTORY, BRAND, SUB)
-        gs, gw = {}, {}
+        gs = keep.tile([P, 3, S], U8, name="gs", align_bytes=64)
+        nc.vector.memset(gs[:].bitcast(I32), 0)
+        spread = over.tile([P, 3, S], U8, name="spread", align_bytes=64, offset=50 * KB)
         for x in order:
-            g = keep.tile([P, S], U8, name=f"gs{x}", align_bytes=64)
-            nc.vector.tensor_copy(g[:], tsc[:].indirect(lists[x][:]))
-            gs[x] = g
+            nc.vector.tensor_copy(spread[:, x, :], tsc[:].indirect(lists[x][:]))
+        raw = {}
+
+        def move_scales(a, r):
+            first = 64 * a + 4 * r
+            nc.sync.dma_start(gs[4 * a + r : P : 32].bitcast(I32), spread[first : first + 49 : 16].bitcast(I32))
+
+        def load_w1(b, a):
+            r = over.tile([P, PACK, PASS], F32, name=f"raw{b}{a}", align_bytes=64, offset=16 * KB * b + 8 * KB * a)
+            nc.sync.dma_start(r[:], w1[a * PASS : (a + 1) * PASS, b * PASS : (b + 1) * PASS].rearrange("(p i) c -> p i c", i=PACK))
+            raw[b, a] = r
+
+        moves = [(a, r) for a in range(KP) for r in range(4)]
+        for a, r in moves[:6]:
+            move_scales(a, r)
+        load_w1(0, 0)
+        for a, r in moves[6:]:
+            move_scales(a, r)
+        load_w1(0, 1)
+        gw = {}
         for a in range(KP):
             for x in order:
                 g = keep.tile([P, S], U32, name=f"gw{x}{a}", align_bytes=64)
                 nc.vector.tensor_copy(g[:], tw[a][:].indirect(lists[x][:]))
                 gw[x, a] = g
+            load_w1(a + 1, 0)
+            load_w1(a + 1, 1)
+            if a == 0:
+                w4c = over.tile([P, HP, 2 * N], U8, name="w4c", align_bytes=64, offset=48 * KB)
+                nc.sync.dma_start(w4c[:].bitcast(I32), w4_words.rearrange("a p c -> p a c").bitcast(I32))
+                w4s = over.tile([P, HP, N], U8, name="w4s", align_bytes=64, offset=51 * KB)
+                nc.vector.memset(w4s[:].bitcast(I32), 0)
+                for q in range(4):
+                    nc.sync.dma_start(
+                        w4s[32 * q : 32 * q + 4, :, :].bitcast(I32),
+                        w4_scales[:, 4 * q : 4 * q + 4, :].rearrange("a r c -> r a c").bitcast(I32),
+                    )
 
         grouped, w1c, w1s = {}, {}, {}
 
         def cast_w1(b, a, u, on_vector):
-            g = work.tile([P, 2, P, PACK], BF16, name="w1g", bufs=4, align_bytes=64)
-            src = raw[b, a][:].rearrange("p i (m t) -> p m t i", t=PACK)[:, :, 2 * u : 2 * u + 2, :]
-            dst = g[:].rearrange("p e m i -> p m e i")
+            if b == 0 and u == 0:
+                g = work.tile([P, 2, P, PACK], BF16, name="w1g_first", bufs=1, align_bytes=64)
+            else:
+                g = work.tile([P, 2, P, PACK], BF16, name="w1g", bufs=4, align_bytes=64)
+            src = raw[b, a][:].rearrange("p i (m t) -> p m i t", t=PACK)[:, :, :, 2 * u : 2 * u + 2]
+            dst = g[:].rearrange("p e m i -> p m i e")
             if on_vector:
                 nc.vector.tensor_copy(dst, src)
             else:
@@ -118,7 +135,7 @@ def tile_list_audit_leakage_scores_kernel(tc, tab_words, tab_scales, offs, offs2
                         lhsT=w1c[b, a, u][:, e * P : (e + 1) * P].bitcast(FP8X4),
                         lhsT_scale=w1s[b, a, u][:, e * P : (e + 1) * P],
                         rhs=gw[x, a][:, cols].bitcast(FP8X4),
-                        rhs_scale=gs[x][4 * a : P, cols],
+                        rhs_scale=gs[4 * a : P, x, cols],
                         start=(a == 0 and i == 0),
                         stop=(a == KP - 1 and i == len(ts) - 1),
                     )
@@ -131,25 +148,29 @@ def tile_list_audit_leakage_scores_kernel(tc, tab_words, tab_scales, offs, offs2
 
         def differences(k):
             b, j0, width, ts = steps[k]
+            d = work.tile([P, 2, width, len(ts)], F32, name="dif", bufs=3)
             for y, x in enumerate((BRAND, SUB)):
-                d = work.tile([P, width, len(ts)], F32, name="dif", bufs=6)
-                nc.vector.tensor_tensor(d[:], banks[k, x][:].rearrange("p e n -> p n e"), fs[k][:], ALU.subtract)
-                dif[k, y] = d
+                nc.vector.tensor_tensor(d[:, y], banks[k, x][:].rearrange("p e n -> p n e"), fs[k][:], ALU.subtract)
+            dif[k] = d
 
         def magnitudes(k):
             b, j0, width, ts = steps[k]
             parts = PACK // len(ts)
             if ts[0] == 0:
+                mag[b, j0] = work.tile([P, parts, 2, width, len(ts)], F32, name="mag", bufs=3)
+            dst = mag[b, j0][:, ts[0] // len(ts)]
+            if k < len(steps) - 1:
+                nc.scalar.activation(dst.rearrange("p y n e -> p (y n e)"), dif[k][:].rearrange("p y n e -> p (y n e)"), ACT.Abs)
+            else:
                 for y in range(2):
-                    mag[b, j0, y] = work.tile([P, parts, width, len(ts)], F32, name="mag", bufs=4)
-            for y in range(2):
-                nc.scalar.activation(mag[b, j0, y][:, ts[0] // len(ts)], dif[k, y][:], ACT.Abs)
+                    nc.scalar.activation(dst[:, y], dif[k][:, y], ACT.Abs)
 
         def add_h(k):
             b, j0, width, ts = steps[k]
             h = work.tile([P, width, PACK // len(ts), len(ts)], BF16, name="hb", bufs=2, align_bytes=64)
+            m = mag[b, j0]
             nc.vector.tensor_tensor(
-                h[:], mag[b, j0, 0][:].rearrange("p u n e -> p n u e"), mag[b, j0, 1][:].rearrange("p u n e -> p n u e"), ALU.add
+                h[:], m[:, :, 0].rearrange("p u n e -> p n u e"), m[:, :, 1].rearrange("p u n e -> p n u e"), ALU.add
             )
             hb[b, j0] = h
 
@@ -212,6 +233,9 @@ def tile_list_audit_leakage_scores_kernel(tc, tab_words, tab_scales, offs, offs2
         products(0)
         copy_factory(0)
         products(1)
+        def finishes(k):
+            return 0 <= k < last - 2 and steps[k][3][-1] == PACK - 1
+
         for k in range(len(steps)):
             b = steps[k][0]
             if k + 1 <= last:
@@ -223,23 +247,29 @@ def tile_list_audit_leakage_scores_kernel(tc, tab_words, tab_scales, offs, offs2
             if b + 1 < HP:
                 a2, u2 = ahead[k % 4]
                 cast_w1(b + 1, a2, u2, (b + 1, a2, u2) in on_vector)
-            if k >= 1 and steps[k - 1][3][-1] == PACK - 1:
-                add_h(k - 1)
+            if finishes(k - 2):
+                add_h(k - 2)
             if b + 1 < HP and k % 4 >= 1:
                 quant_w1(b + 1, *ahead[k % 4 - 1])
-            if k >= 2 and steps[k - 2][3][-1] == PACK - 1:
-                quant_h(k - 2)
-                if steps[k - 2][1] == 0:
-                    scores(0, steps[k - 2][0])
-                    scores(1, steps[k - 2][0])
+            if finishes(k - 3):
+                quant_h(k - 3)
+                if steps[k - 3][1] == 0:
+                    scores(0, steps[k - 3][0])
+                    scores(1, steps[k - 3][0])
             if b + 1 < HP and k % 4 == 3:
                 quant_w1(b + 1, 1, 1)
             if k + 2 <= last and steps[k + 2][0] != b:
                 products(k + 2)
             if k == last - 1:
+                add_h(last - 2)
                 for o in (2, 3, 4):
                     scores(o, 0)
                     scores(o, 1)
+            if k == last:
+                add_h(last - 1)
+                quant_h(last - 2)
+                scores(0, HP - 1)
+                scores(1, HP - 1)
         quant_h(last - 1)
         add_h(last)
         scores(2, HP - 1)

@@ -3,7 +3,7 @@ from contextlib import ExitStack
 import concourse.mybir as mybir
 
 K, T, S, H, N = 1024, 4096, 512, 1536, 512
-FLOPS = 2 * K * H * S * 3 + 2 * H * N * S
+FLOPS = 3 * 2 * K * H * S + 2 * H * N * S
 
 F32 = mybir.dt.float32
 BF16 = mybir.dt.bfloat16
@@ -19,265 +19,272 @@ ACT = mybir.ActivationFunctionType
 P = 128
 PACK = 4
 PASS = P * PACK
-KP = K // PASS
-HP = H // PASS
-JH = 256
-JQ = 128
+K_PASSES = K // PASS
+R_BLOCKS = H // PASS
+QUADRANT = 32
+HALF = S // 2
+QUARTER = S // 4
 BRAND, FACTORY, SUB = 0, 1, 2
+LISTS = (FACTORY, BRAND, SUB)
+RAW_BYTES = PACK * PASS * 4
+TABLE_BYTES = T * 4
 
 
 def tile_list_audit_leakage_scores_kernel(tc, tab_words, tab_scales, offs, offs2, offs3, w1, w4_words, w4_scales, out):
     nc = tc.nc
     with ExitStack() as ctx:
         keep = ctx.enter_context(tc.tile_pool(name="keep", bufs=1))
-        over = ctx.enter_context(tc.tile_pool(name="over", bufs=1))
+        reused = ctx.enter_context(tc.tile_pool(name="reused", bufs=1))
         work = ctx.enter_context(tc.tile_pool(name="work", bufs=2))
         psum = ctx.enter_context(tc.psum_pool(name="psum", bufs=1))
 
-        KB = 1024
-        tsc = over.tile([P, T], U8, name="tsc", align_bytes=64, offset=6 * KB)
-        nc.vector.memset(tsc[:].bitcast(I32), 0)
+        tab_s = reused.tile([P, T], U8, name="tab_s", align_bytes=64, offset=RAW_BYTES - T // 2)
+        nc.vector.memset(tab_s[:].bitcast(I32), 0)
         lists = []
         for x, src in enumerate((offs, offs2, offs3)):
             lst = keep.tile([P, S // 16], U16, name=f"list{x}")
             nc.sync.dma_start(lst[:], src)
             lists.append(lst)
-        nc.sync.dma_start(tsc[0:P:4, :].bitcast(I32), tab_scales.rearrange("a q t -> (a q) t").bitcast(I32))
+        nc.sync.dma_start(tab_s[0:P:PACK, :].bitcast(I32), tab_scales.rearrange("a q t -> (a q) t").bitcast(I32))
 
-        tw = []
-        for a in range(KP):
-            t = over.tile([P, T], U32, name=f"tw{a}", align_bytes=64, offset=16 * KB * (a + 1))
-            nc.sync.dma_start(t[:].bitcast(I32), tab_words[a].rearrange("p t i -> p (t i)").bitcast(I32))
-            tw.append(t)
+        tab_w = []
+        for a in range(K_PASSES):
+            words = reused.tile([P, T], U32, name=f"tab_w{a}", align_bytes=64, offset=TABLE_BYTES * (a + 1))
+            nc.sync.dma_start(words[:].bitcast(I32), tab_words[a].rearrange("p t i -> p (t i)").bitcast(I32))
+            tab_w.append(words)
 
-        order = (FACTORY, BRAND, SUB)
-        gs = keep.tile([P, 3, S], U8, name="gs", align_bytes=64)
-        nc.vector.memset(gs[:].bitcast(I32), 0)
-        spread = over.tile([P, 3, S], U8, name="spread", align_bytes=64, offset=50 * KB)
-        for x in order:
-            nc.vector.tensor_copy(spread[:, x, :], tsc[:].indirect(lists[x][:]))
+        got_s = []
+        for a in range(K_PASSES):
+            plane = keep.tile([P, 3, S], U8, name=f"got_s{a}", align_bytes=64)
+            nc.vector.memset(plane[:].bitcast(I32), 0)
+            got_s.append(plane)
+        spread_s = keep.tile([P, 3, S], U8, name="spread_s", align_bytes=64)
+        for x in LISTS:
+            nc.vector.tensor_copy(spread_s[:, x, :], tab_s[:].indirect(lists[x][:]))
+
+        def move_scales(a):
+            for r in range(PACK):
+                first = 64 * a + 4 * r
+                nc.sync.dma_start(
+                    got_s[a][r:P:QUADRANT].bitcast(I32), spread_s[first : first + 3 * 16 + 1 : 16].bitcast(I32)
+                )
+
         raw = {}
 
-        def move_scales(a, r):
-            first = 64 * a + 4 * r
-            nc.sync.dma_start(gs[4 * a + r : P : 32].bitcast(I32), spread[first : first + 49 : 16].bitcast(I32))
+        def load_w1(b):
+            for a in range(K_PASSES):
+                raw[b, a] = reused.tile(
+                    [P, PACK, PASS], F32, name=f"raw{b}{a}", align_bytes=64, offset=TABLE_BYTES * b + RAW_BYTES * a
+                )
+                rows = w1[a * PASS : (a + 1) * PASS, b * PASS : (b + 1) * PASS]
+                nc.sync.dma_start(raw[b, a][:], rows.rearrange("(p i) c -> p i c", i=PACK))
 
-        def load_w1(b, a):
-            r = over.tile([P, PACK, PASS], F32, name=f"raw{b}{a}", align_bytes=64, offset=16 * KB * b + 8 * KB * a)
-            nc.sync.dma_start(r[:], w1[a * PASS : (a + 1) * PASS, b * PASS : (b + 1) * PASS].rearrange("(p i) c -> p i c", i=PACK))
-            raw[b, a] = r
+        move_scales(0)
+        load_w1(0)
+        move_scales(1)
 
-        moves = [(a, r) for a in range(KP) for r in range(4)]
-        for a, r in moves[:6]:
-            move_scales(a, r)
-        load_w1(0, 0)
-        for a, r in moves[6:]:
-            move_scales(a, r)
-        load_w1(0, 1)
-        gw = {}
-        for a in range(KP):
-            for x in order:
-                g = keep.tile([P, S], U32, name=f"gw{x}{a}", align_bytes=64)
-                nc.vector.tensor_copy(g[:], tw[a][:].indirect(lists[x][:]))
-                gw[x, a] = g
-            load_w1(a + 1, 0)
-            load_w1(a + 1, 1)
-            if a == 0:
-                w4c = over.tile([P, HP, 2 * N], U8, name="w4c", align_bytes=64, offset=48 * KB)
-                nc.sync.dma_start(w4c[:].bitcast(I32), w4_words.rearrange("a p c -> p a c").bitcast(I32))
-                w4s = over.tile([P, HP, N], U8, name="w4s", align_bytes=64, offset=51 * KB)
-                nc.vector.memset(w4s[:].bitcast(I32), 0)
-                for q in range(4):
-                    nc.sync.dma_start(
-                        w4s[32 * q : 32 * q + 4, :, :].bitcast(I32),
-                        w4_scales[:, 4 * q : 4 * q + 4, :].rearrange("a r c -> r a c").bitcast(I32),
-                    )
+        got_w = {}
+        for a in range(K_PASSES):
+            for x in LISTS:
+                got_w[x, a] = keep.tile([P, S], U32, name=f"got_w{x}{a}", align_bytes=64)
+                nc.vector.tensor_copy(got_w[x, a][:], tab_w[a][:].indirect(lists[x][:]))
+            load_w1(a + 1)
 
-        grouped, w1c, w1s = {}, {}, {}
+        rounded, w1_c, w1_s = {}, {}, {}
 
-        def cast_w1(b, a, u, on_vector):
+        def round_w1(b, a, u, on_vector):
             if b == 0 and u == 0:
-                g = work.tile([P, 2, P, PACK], BF16, name="w1g_first", bufs=1, align_bytes=64)
+                tile = work.tile([P, 2, P, PACK], BF16, name="rounded_first", bufs=1, align_bytes=64)
             else:
-                g = work.tile([P, 2, P, PACK], BF16, name="w1g", bufs=4, align_bytes=64)
+                tile = work.tile([P, 2, P, PACK], BF16, name="rounded", bufs=4, align_bytes=64)
             src = raw[b, a][:].rearrange("p i (m t) -> p m i t", t=PACK)[:, :, :, 2 * u : 2 * u + 2]
-            dst = g[:].rearrange("p e m i -> p m i e")
+            dst = tile[:].rearrange("p e m i -> p m i e")
             if on_vector:
                 nc.vector.tensor_copy(dst, src)
             else:
                 nc.scalar.copy(dst, src)
-            grouped[b, a, u] = g
+            rounded[b, a, u] = tile
 
-        def quant_w1(b, a, u):
-            c = keep.tile([P, 2 * P], U32, name=f"w1c{b}{a}{u}", align_bytes=64)
-            s = keep.tile([P, 2 * P], U8, name=f"w1s{b}{a}{u}", align_bytes=64)
-            nc.vector.quantize_mx(out=c[:].bitcast(FP8X4), scales=s[:], in_=grouped[b, a, u][:].rearrange("p e m i -> p (e m i)"))
-            w1c[b, a, u], w1s[b, a, u] = c, s
+        def quantise_w1(b, a, u):
+            w1_c[b, a, u] = keep.tile([P, 2 * P], U32, name=f"w1_c{b}{a}{u}", align_bytes=64)
+            w1_s[b, a, u] = keep.tile([P, 2 * P], U8, name=f"w1_s{b}{a}{u}", align_bytes=64)
+            nc.vector.quantize_mx(
+                out=w1_c[b, a, u][:].bitcast(FP8X4),
+                scales=w1_s[b, a, u][:],
+                in_=rounded[b, a, u][:].rearrange("p e m i -> p (e m i)"),
+            )
 
-        steps = [(b, jh * JH, JH, (2 * u, 2 * u + 1)) for b in range(HP) for jh in range(2) for u in range(2)][:-2]
-        steps = steps + [(HP - 1, JH + c * JQ, JQ, (0, 1, 2, 3)) for c in range(2)]
-        banks, fs, dif, mag, hb, hc, hs = {}, {}, {}, {}, {}, {}, {}
+        units = [(0, 0), (0, HALF), (1, 0), (2, 0), (1, HALF)]
+        steps = [(b, j0, HALF, (2 * u, 2 * u + 1)) for b, j0 in units for u in range(2)]
+        steps = steps + [(R_BLOCKS - 1, HALF + c * QUARTER, QUARTER, (0, 1, 2, 3)) for c in range(2)]
+        last = len(steps) - 1
+        banks, factory, diffs, mags, h_bf, h_c, h_s = {}, {}, {}, {}, {}, {}, {}
 
         def products(k):
-            b, j0, width, ts = steps[k]
+            b, j0, width, slots = steps[k]
             cols = slice(j0, j0 + width)
-            for x in order:
-                banks[k, x] = psum.tile([P, len(ts), width], F32, name=f"bank{x}", bufs=2)
+            for x in LISTS:
+                banks[k, x] = psum.tile([P, len(slots), width], F32, name=f"bank{x}", bufs=2)
             if k == 0:
-                seq = [(x, a) for a in range(KP) for x in order]
+                sequence = [(x, a) for a in range(K_PASSES) for x in LISTS]
             else:
-                seq = [(x, a) for x in order for a in range(KP)]
-            for x, a in seq:
-                for i, t in enumerate(ts):
+                sequence = [(x, a) for x in LISTS for a in range(K_PASSES)]
+            for x, a in sequence:
+                for n, t in enumerate(slots):
                     u, e = divmod(t, 2)
                     nc.tensor.matmul_mx(
-                        out=banks[k, x][:, i, :],
-                        lhsT=w1c[b, a, u][:, e * P : (e + 1) * P].bitcast(FP8X4),
-                        lhsT_scale=w1s[b, a, u][:, e * P : (e + 1) * P],
-                        rhs=gw[x, a][:, cols].bitcast(FP8X4),
-                        rhs_scale=gs[4 * a : P, x, cols],
-                        start=(a == 0 and i == 0),
-                        stop=(a == KP - 1 and i == len(ts) - 1),
+                        out=banks[k, x][:, n, :],
+                        lhsT=w1_c[b, a, u][:, e * P : (e + 1) * P].bitcast(FP8X4),
+                        lhsT_scale=w1_s[b, a, u][:, e * P : (e + 1) * P],
+                        rhs=got_w[x, a][:, cols].bitcast(FP8X4),
+                        rhs_scale=got_s[a][:, x, cols],
+                        start=(a == 0 and n == 0),
+                        stop=(a == K_PASSES - 1 and n == len(slots) - 1),
                     )
 
         def copy_factory(k):
-            b, j0, width, ts = steps[k]
-            f = work.tile([P, width, len(ts)], F32, name="fs", bufs=3)
-            nc.scalar.copy(f[:], banks[k, FACTORY][:].rearrange("p e n -> p n e"))
-            fs[k] = f
+            b, j0, width, slots = steps[k]
+            factory[k] = work.tile([P, width, len(slots)], F32, name="factory", bufs=3)
+            nc.scalar.copy(factory[k][:], banks[k, FACTORY][:].rearrange("p t j -> p j t"))
 
         def differences(k):
-            b, j0, width, ts = steps[k]
-            d = work.tile([P, 2, width, len(ts)], F32, name="dif", bufs=3)
+            b, j0, width, slots = steps[k]
+            diffs[k] = work.tile([P, 2, width, len(slots)], F32, name="diffs", bufs=3)
             for y, x in enumerate((BRAND, SUB)):
-                nc.vector.tensor_tensor(d[:, y], banks[k, x][:].rearrange("p e n -> p n e"), fs[k][:], ALU.subtract)
-            dif[k] = d
+                nc.vector.tensor_tensor(diffs[k][:, y], banks[k, x][:].rearrange("p t j -> p j t"), factory[k][:], ALU.subtract)
 
         def magnitudes(k):
-            b, j0, width, ts = steps[k]
-            parts = PACK // len(ts)
-            if ts[0] == 0:
-                mag[b, j0] = work.tile([P, parts, 2, width, len(ts)], F32, name="mag", bufs=3)
-            dst = mag[b, j0][:, ts[0] // len(ts)]
-            if k < len(steps) - 1:
-                nc.scalar.activation(dst.rearrange("p y n e -> p (y n e)"), dif[k][:].rearrange("p y n e -> p (y n e)"), ACT.Abs)
+            b, j0, width, slots = steps[k]
+            if slots[0] == 0:
+                mags[b, j0] = work.tile([P, PACK // len(slots), 2, width, len(slots)], F32, name="mags", bufs=3)
+            dst = mags[b, j0][:, slots[0] // len(slots)]
+            if k < last:
+                nc.scalar.activation(dst.rearrange("p y j t -> p (y j t)"), diffs[k][:].rearrange("p y j t -> p (y j t)"), ACT.Abs)
             else:
                 for y in range(2):
-                    nc.scalar.activation(dst[:, y], dif[k][:, y], ACT.Abs)
+                    nc.scalar.activation(dst[:, y], diffs[k][:, y], ACT.Abs)
 
         def add_h(k):
-            b, j0, width, ts = steps[k]
-            h = work.tile([P, width, PACK // len(ts), len(ts)], BF16, name="hb", bufs=2, align_bytes=64)
-            m = mag[b, j0]
+            b, j0, width, slots = steps[k]
+            h_bf[b, j0] = work.tile([P, width, PACK // len(slots), len(slots)], BF16, name="h_bf", bufs=2, align_bytes=64)
+            both = mags[b, j0]
             nc.vector.tensor_tensor(
-                h[:], m[:, :, 0].rearrange("p u n e -> p n u e"), m[:, :, 1].rearrange("p u n e -> p n u e"), ALU.add
+                h_bf[b, j0][:], both[:, :, 0].rearrange("p u j e -> p j u e"), both[:, :, 1].rearrange("p u j e -> p j u e"), ALU.add
             )
-            hb[b, j0] = h
 
-        def quant_h(k):
-            b, j0, width, ts = steps[k]
-            c = keep.tile([P, width], U32, name=f"hc{b}{j0}", align_bytes=64)
-            s = keep.tile([P, width], U8, name=f"hs{b}{j0}", align_bytes=64)
-            nc.vector.quantize_mx(out=c[:].bitcast(FP8X4), scales=s[:], in_=hb[b, j0][:].rearrange("p n u e -> p (n u e)"))
-            hc[b, j0], hs[b, j0] = c, s
+        def quantise_h(k):
+            b, j0, width, slots = steps[k]
+            h_c[b, j0] = keep.tile([P, width], U32, name=f"h_c{b}{j0}", align_bytes=64)
+            h_s[b, j0] = keep.tile([P, width], U8, name=f"h_s{b}{j0}", align_bytes=64)
+            nc.vector.quantize_mx(
+                out=h_c[b, j0][:].bitcast(FP8X4), scales=h_s[b, j0][:], in_=h_bf[b, j0][:].rearrange("p j u e -> p (j u e)")
+            )
 
-        outs = [
-            (0, JH, (0, 1), "obank0", 1),
-            (0, JH, (2, 3), "obank1", 1),
-            (JH, JQ, (0, 1, 2, 3), f"bank{FACTORY}", 2),
-            (JH + JQ, JQ, (0, 1), f"bank{BRAND}", 2),
-            (JH + JQ, JQ, (2, 3), f"bank{SUB}", 2),
+        score_banks = [
+            (0, HALF, (0, 1), "scores0", 1),
+            (0, HALF, (2, 3), "scores1", 1),
+            (HALF, QUARTER, (0, 1, 2, 3), f"bank{FACTORY}", 2),
+            (HALF + QUARTER, QUARTER, (0, 1), f"bank{BRAND}", 2),
+            (HALF + QUARTER, QUARTER, (2, 3), f"bank{SUB}", 2),
         ]
-        obank = {}
+        FIRST_HALF, SECOND_HALF = (0, 1), (2, 3, 4)
+        sums = {}
 
         def scores(o, b):
-            j0, width, ys, tag, depth = outs[o]
+            j0, width, row_tiles, tag, depth = score_banks[o]
             if b == 0:
-                obank[o] = psum.tile([P, len(ys), width], F32, name=tag, bufs=depth)
-            base = j0 if (b, j0) in hc else JH
-            cols = slice(j0 - base, j0 - base + width)
-            for i, y in enumerate(ys):
+                sums[o] = psum.tile([P, len(row_tiles), width], F32, name=tag, bufs=depth)
+            unit_j0 = j0 if (b, j0) in h_c else HALF
+            cols = slice(j0 - unit_j0, j0 - unit_j0 + width)
+            for n, y in enumerate(row_tiles):
                 nc.tensor.matmul_mx(
-                    out=obank[o][:, i, :],
-                    lhsT=w4c[:, b, 2 * y * P : 2 * (y + 1) * P].bitcast(FP4X4),
-                    lhsT_scale=w4s[:, b, y * P : (y + 1) * P],
-                    rhs=hc[b, base][:, cols].bitcast(FP8X4),
-                    rhs_scale=hs[b, base][:, cols],
-                    start=(b == 0 and i == 0),
-                    stop=(b == HP - 1 and i == len(ys) - 1),
+                    out=sums[o][:, n, :],
+                    lhsT=w4_c[:, b, 2 * y * P : 2 * (y + 1) * P].bitcast(FP4X4),
+                    lhsT_scale=w4_s[:, b, y * P : (y + 1) * P],
+                    rhs=h_c[b, unit_j0][:, cols].bitcast(FP8X4),
+                    rhs_scale=h_s[b, unit_j0][:, cols],
+                    start=(b == 0 and n == 0),
+                    stop=(b == R_BLOCKS - 1 and n == len(row_tiles) - 1),
                 )
 
         def store(o, on_vector):
-            j0, width, ys, tag, depth = outs[o]
-            res = work.tile([P, len(ys), width], F32, name="res", bufs=5)
+            j0, width, row_tiles, tag, depth = score_banks[o]
+            result = work.tile([P, len(row_tiles), width], F32, name="result", bufs=len(score_banks))
             if on_vector:
-                nc.vector.tensor_copy(res[:], obank[o][:])
+                nc.vector.tensor_copy(result[:], sums[o][:])
             else:
-                nc.scalar.copy(res[:], obank[o][:])
-            rows = out[ys[0] * P : (ys[-1] + 1) * P, j0 : j0 + width]
-            nc.sync.dma_start(rows.rearrange("(y p) c -> p y c", p=P), res[:])
+                nc.scalar.copy(result[:], sums[o][:])
+            rows = out[row_tiles[0] * P : (row_tiles[-1] + 1) * P, j0 : j0 + width]
+            nc.sync.dma_start(rows.rearrange("(y p) c -> p y c", p=P), result[:])
 
-        cast_w1(0, 0, 0, False)
-        cast_w1(0, 0, 1, False)
-        quant_w1(0, 0, 0)
-        cast_w1(0, 1, 0, True)
-        cast_w1(0, 1, 1, False)
-        quant_w1(0, 1, 0)
-        quant_w1(0, 0, 1)
-        quant_w1(0, 1, 1)
+        round_w1(0, 0, 0, False)
+        round_w1(0, 0, 1, False)
+        quantise_w1(0, 0, 0)
+        round_w1(0, 1, 0, True)
+        round_w1(0, 1, 1, False)
+        quantise_w1(0, 1, 0)
+        quantise_w1(0, 0, 1)
+        quantise_w1(0, 1, 1)
 
-        ahead = ((0, 0), (1, 0), (0, 1), (1, 1))
-        on_vector = {(1, 1, 0), (1, 1, 1), (2, 1, 0)}
+        w4_c = reused.tile([P, R_BLOCKS, 2 * N], U8, name="w4_c", align_bytes=64, offset=0)
+        nc.sync.dma_start(w4_c[:].bitcast(I32), w4_words.rearrange("b p c -> p b c").bitcast(I32))
+        w4_s = reused.tile([P, R_BLOCKS, N], U8, name="w4_s", align_bytes=64, offset=R_BLOCKS * 2 * N)
+        nc.vector.memset(w4_s[:].bitcast(I32), 0)
+        for q in range(P // QUADRANT):
+            nc.sync.dma_start(
+                w4_s[QUADRANT * q : QUADRANT * q + PACK].bitcast(I32),
+                w4_scales[:, PACK * q : PACK * (q + 1), :].rearrange("b r c -> r b c").bitcast(I32),
+            )
 
-        last = len(steps) - 1
+        pairs = [(b, a, u) for b in range(1, R_BLOCKS) for u in range(2) for a in range(K_PASSES)]
+
+        ADD_LAG, QUANT_LAG = 2, 3
+        lagged = [k for k in range(1, last - 2, 2)]
+
         products(0)
         copy_factory(0)
         products(1)
-        def finishes(k):
-            return 0 <= k < last - 2 and steps[k][3][-1] == PACK - 1
-
         for k in range(len(steps)):
-            b = steps[k][0]
-            if k + 1 <= last:
+            ahead = k + 2
+            weights_ready = ahead <= last and all((steps[ahead][0], a, t // 2) in w1_c for a in range(K_PASSES) for t in steps[ahead][3])
+            if k < last:
                 copy_factory(k + 1)
             differences(k)
-            if k + 2 <= last and steps[k + 2][0] == b:
-                products(k + 2)
+            if weights_ready:
+                products(ahead)
             magnitudes(k)
-            if b + 1 < HP:
-                a2, u2 = ahead[k % 4]
-                cast_w1(b + 1, a2, u2, (b + 1, a2, u2) in on_vector)
-            if finishes(k - 2):
-                add_h(k - 2)
-            if b + 1 < HP and k % 4 >= 1:
-                quant_w1(b + 1, *ahead[k % 4 - 1])
-            if finishes(k - 3):
-                quant_h(k - 3)
-                if steps[k - 3][1] == 0:
-                    scores(0, steps[k - 3][0])
-                    scores(1, steps[k - 3][0])
-            if b + 1 < HP and k % 4 == 3:
-                quant_w1(b + 1, 1, 1)
-            if k + 2 <= last and steps[k + 2][0] != b:
-                products(k + 2)
+            for n, pair in enumerate(pairs):
+                if (n + 1) // 2 == k:
+                    round_w1(*pair, n % 2 == 0)
+            if k - ADD_LAG in lagged:
+                add_h(k - ADD_LAG)
+            for n, pair in enumerate(pairs):
+                if (n + 1) // 2 == k - 1:
+                    quantise_w1(*pair)
+            if ahead <= last and not weights_ready:
+                products(ahead)
+            if k - QUANT_LAG in lagged:
+                quantise_h(k - QUANT_LAG)
+                done_b, done_j0 = steps[k - QUANT_LAG][:2]
+                if done_j0 == 0:
+                    for o in FIRST_HALF:
+                        scores(o, done_b)
             if k == last - 1:
                 add_h(last - 2)
-                for o in (2, 3, 4):
+                for o in SECOND_HALF:
                     scores(o, 0)
-                    scores(o, 1)
-            if k == last:
-                add_h(last - 1)
-                quant_h(last - 2)
-                scores(0, HP - 1)
-                scores(1, HP - 1)
-        quant_h(last - 1)
+                store(0, False)
+        quantise_h(last - 2)
+        add_h(last - 1)
+        for o in SECOND_HALF:
+            scores(o, 1)
+        quantise_h(last - 1)
         add_h(last)
-        scores(2, HP - 1)
-        store(0, False)
-        quant_h(last)
-        scores(3, HP - 1)
-        scores(4, HP - 1)
-        store(1, True)
+        scores(2, R_BLOCKS - 1)
+        store(1, False)
+        quantise_h(last)
+        scores(3, R_BLOCKS - 1)
+        scores(4, R_BLOCKS - 1)
         store(2, False)
         store(3, False)
         store(4, True)

from contextlib import ExitStack

import concourse.mybir as mybir

K, T, S, H, N = 1024, 4096, 512, 1536, 512
FLOPS = 3 * 2 * K * H * S + 2 * H * N * S

F32 = mybir.dt.float32
BF16 = mybir.dt.bfloat16
I32 = mybir.dt.int32
U32 = mybir.dt.uint32
U16 = mybir.dt.uint16
U8 = mybir.dt.uint8
FP8X4 = mybir.dt.float8_e4m3fn_x4
FP4X4 = mybir.dt.float4_e2m1fn_x4
ALU = mybir.AluOpType
ACT = mybir.ActivationFunctionType

P = 128
PACK = 4
PASS = P * PACK
K_PASSES = K // PASS
R_BLOCKS = H // PASS
QUADRANT = 32
HALF = S // 2
QUARTER = S // 4
BRAND, FACTORY, SUB = 0, 1, 2
LISTS = (FACTORY, BRAND, SUB)
RAW_BYTES = PACK * PASS * 4
TABLE_BYTES = T * 4


def tile_list_audit_leakage_scores_kernel(tc, tab_words, tab_scales, offs, offs2, offs3, w1, w4_words, w4_scales, out):
    nc = tc.nc
    with ExitStack() as ctx:
        keep = ctx.enter_context(tc.tile_pool(name="keep", bufs=1))
        reused = ctx.enter_context(tc.tile_pool(name="reused", bufs=1))
        work = ctx.enter_context(tc.tile_pool(name="work", bufs=2))
        psum = ctx.enter_context(tc.psum_pool(name="psum", bufs=1))

        tab_s = reused.tile([P, T], U8, name="tab_s", align_bytes=64, offset=RAW_BYTES - T // 2)
        nc.vector.memset(tab_s[:].bitcast(I32), 0)
        lists = []
        for x, src in enumerate((offs, offs2, offs3)):
            lst = keep.tile([P, S // 16], U16, name=f"list{x}")
            nc.sync.dma_start(lst[:], src)
            lists.append(lst)
        nc.sync.dma_start(tab_s[0:P:PACK, :].bitcast(I32), tab_scales.rearrange("a q t -> (a q) t").bitcast(I32))

        tab_w = []
        for a in range(K_PASSES):
            words = reused.tile([P, T], U32, name=f"tab_w{a}", align_bytes=64, offset=TABLE_BYTES * (a + 1))
            nc.sync.dma_start(words[:].bitcast(I32), tab_words[a].rearrange("p t i -> p (t i)").bitcast(I32))
            tab_w.append(words)

        got_s = []
        for a in range(K_PASSES):
            plane = keep.tile([P, 3, S], U8, name=f"got_s{a}", align_bytes=64)
            nc.vector.memset(plane[:].bitcast(I32), 0)
            got_s.append(plane)
        spread_s = keep.tile([P, 3, S], U8, name="spread_s", align_bytes=64)
        for x in LISTS:
            nc.vector.tensor_copy(spread_s[:, x, :], tab_s[:].indirect(lists[x][:]))

        def move_scales(a):
            for r in range(PACK):
                first = 64 * a + 4 * r
                nc.sync.dma_start(
                    got_s[a][r:P:QUADRANT].bitcast(I32), spread_s[first : first + 3 * 16 + 1 : 16].bitcast(I32)
                )

        raw = {}

        def load_w1(b):
            for a in range(K_PASSES):
                raw[b, a] = reused.tile(
                    [P, PACK, PASS], F32, name=f"raw{b}{a}", align_bytes=64, offset=TABLE_BYTES * b + RAW_BYTES * a
                )
                rows = w1[a * PASS : (a + 1) * PASS, b * PASS : (b + 1) * PASS]
                nc.sync.dma_start(raw[b, a][:], rows.rearrange("(p i) c -> p i c", i=PACK))

        move_scales(0)
        load_w1(0)
        move_scales(1)

        got_w = {}
        for a in range(K_PASSES):
            for x in LISTS:
                got_w[x, a] = keep.tile([P, S], U32, name=f"got_w{x}{a}", align_bytes=64)
                nc.vector.tensor_copy(got_w[x, a][:], tab_w[a][:].indirect(lists[x][:]))
            load_w1(a + 1)

        rounded, w1_c, w1_s = {}, {}, {}

        def round_w1(b, a, u, on_vector):
            if b == 0 and u == 0:
                tile = work.tile([P, 2, P, PACK], BF16, name="rounded_first", bufs=1, align_bytes=64)
            else:
                tile = work.tile([P, 2, P, PACK], BF16, name="rounded", bufs=4, align_bytes=64)
            src = raw[b, a][:].rearrange("p i (m t) -> p m i t", t=PACK)[:, :, :, 2 * u : 2 * u + 2]
            dst = tile[:].rearrange("p e m i -> p m i e")
            if on_vector:
                nc.vector.tensor_copy(dst, src)
            else:
                nc.scalar.copy(dst, src)
            rounded[b, a, u] = tile

        def quantise_w1(b, a, u):
            w1_c[b, a, u] = keep.tile([P, 2 * P], U32, name=f"w1_c{b}{a}{u}", align_bytes=64)
            w1_s[b, a, u] = keep.tile([P, 2 * P], U8, name=f"w1_s{b}{a}{u}", align_bytes=64)
            nc.vector.quantize_mx(
                out=w1_c[b, a, u][:].bitcast(FP8X4),
                scales=w1_s[b, a, u][:],
                in_=rounded[b, a, u][:].rearrange("p e m i -> p (e m i)"),
            )

        units = [(0, 0), (0, HALF), (1, 0), (2, 0), (1, HALF)]
        steps = [(b, j0, HALF, (2 * u, 2 * u + 1)) for b, j0 in units for u in range(2)]
        steps = steps + [(R_BLOCKS - 1, HALF + c * QUARTER, QUARTER, (0, 1, 2, 3)) for c in range(2)]
        last = len(steps) - 1
        banks, factory, diffs, mags, h_bf, h_c, h_s = {}, {}, {}, {}, {}, {}, {}

        def products(k):
            b, j0, width, slots = steps[k]
            cols = slice(j0, j0 + width)
            for x in LISTS:
                banks[k, x] = psum.tile([P, len(slots), width], F32, name=f"bank{x}", bufs=2)
            if k == 0:
                sequence = [(x, a) for a in range(K_PASSES) for x in LISTS]
            else:
                sequence = [(x, a) for x in LISTS for a in range(K_PASSES)]
            for x, a in sequence:
                for n, t in enumerate(slots):
                    u, e = divmod(t, 2)
                    nc.tensor.matmul_mx(
                        out=banks[k, x][:, n, :],
                        lhsT=w1_c[b, a, u][:, e * P : (e + 1) * P].bitcast(FP8X4),
                        lhsT_scale=w1_s[b, a, u][:, e * P : (e + 1) * P],
                        rhs=got_w[x, a][:, cols].bitcast(FP8X4),
                        rhs_scale=got_s[a][:, x, cols],
                        start=(a == 0 and n == 0),
                        stop=(a == K_PASSES - 1 and n == len(slots) - 1),
                    )

        def copy_factory(k):
            b, j0, width, slots = steps[k]
            factory[k] = work.tile([P, width, len(slots)], F32, name="factory", bufs=3)
            nc.scalar.copy(factory[k][:], banks[k, FACTORY][:].rearrange("p t j -> p j t"))

        def differences(k):
            b, j0, width, slots = steps[k]
            diffs[k] = work.tile([P, 2, width, len(slots)], F32, name="diffs", bufs=3)
            for y, x in enumerate((BRAND, SUB)):
                nc.vector.tensor_tensor(diffs[k][:, y], banks[k, x][:].rearrange("p t j -> p j t"), factory[k][:], ALU.subtract)

        def magnitudes(k):
            b, j0, width, slots = steps[k]
            if slots[0] == 0:
                mags[b, j0] = work.tile([P, PACK // len(slots), 2, width, len(slots)], F32, name="mags", bufs=3)
            dst = mags[b, j0][:, slots[0] // len(slots)]
            if k < last:
                nc.scalar.activation(dst.rearrange("p y j t -> p (y j t)"), diffs[k][:].rearrange("p y j t -> p (y j t)"), ACT.Abs)
            else:
                for y in range(2):
                    nc.scalar.activation(dst[:, y], diffs[k][:, y], ACT.Abs)

        def add_h(k):
            b, j0, width, slots = steps[k]
            h_bf[b, j0] = work.tile([P, width, PACK // len(slots), len(slots)], BF16, name="h_bf", bufs=2, align_bytes=64)
            both = mags[b, j0]
            nc.vector.tensor_tensor(
                h_bf[b, j0][:], both[:, :, 0].rearrange("p u j e -> p j u e"), both[:, :, 1].rearrange("p u j e -> p j u e"), ALU.add
            )

        def quantise_h(k):
            b, j0, width, slots = steps[k]
            h_c[b, j0] = keep.tile([P, width], U32, name=f"h_c{b}{j0}", align_bytes=64)
            h_s[b, j0] = keep.tile([P, width], U8, name=f"h_s{b}{j0}", align_bytes=64)
            nc.vector.quantize_mx(
                out=h_c[b, j0][:].bitcast(FP8X4), scales=h_s[b, j0][:], in_=h_bf[b, j0][:].rearrange("p j u e -> p (j u e)")
            )

        score_banks = [
            (0, HALF, (0, 1), "scores0", 1),
            (0, HALF, (2, 3), "scores1", 1),
            (HALF, QUARTER, (0, 1, 2, 3), f"bank{FACTORY}", 2),
            (HALF + QUARTER, QUARTER, (0, 1), f"bank{BRAND}", 2),
            (HALF + QUARTER, QUARTER, (2, 3), f"bank{SUB}", 2),
        ]
        FIRST_HALF, SECOND_HALF = (0, 1), (2, 3, 4)
        sums = {}

        def scores(o, b):
            j0, width, row_tiles, tag, depth = score_banks[o]
            if b == 0:
                sums[o] = psum.tile([P, len(row_tiles), width], F32, name=tag, bufs=depth)
            unit_j0 = j0 if (b, j0) in h_c else HALF
            cols = slice(j0 - unit_j0, j0 - unit_j0 + width)
            for n, y in enumerate(row_tiles):
                nc.tensor.matmul_mx(
                    out=sums[o][:, n, :],
                    lhsT=w4_c[:, b, 2 * y * P : 2 * (y + 1) * P].bitcast(FP4X4),
                    lhsT_scale=w4_s[:, b, y * P : (y + 1) * P],
                    rhs=h_c[b, unit_j0][:, cols].bitcast(FP8X4),
                    rhs_scale=h_s[b, unit_j0][:, cols],
                    start=(b == 0 and n == 0),
                    stop=(b == R_BLOCKS - 1 and n == len(row_tiles) - 1),
                )

        def store(o, on_vector):
            j0, width, row_tiles, tag, depth = score_banks[o]
            result = work.tile([P, len(row_tiles), width], F32, name="result", bufs=len(score_banks))
            if on_vector:
                nc.vector.tensor_copy(result[:], sums[o][:])
            else:
                nc.scalar.copy(result[:], sums[o][:])
            rows = out[row_tiles[0] * P : (row_tiles[-1] + 1) * P, j0 : j0 + width]
            nc.sync.dma_start(rows.rearrange("(y p) c -> p y c", p=P), result[:])

        round_w1(0, 0, 0, False)
        round_w1(0, 0, 1, False)
        quantise_w1(0, 0, 0)
        round_w1(0, 1, 0, True)
        round_w1(0, 1, 1, False)
        quantise_w1(0, 1, 0)
        quantise_w1(0, 0, 1)
        quantise_w1(0, 1, 1)

        w4_c = reused.tile([P, R_BLOCKS, 2 * N], U8, name="w4_c", align_bytes=64, offset=0)
        nc.sync.dma_start(w4_c[:].bitcast(I32), w4_words.rearrange("b p c -> p b c").bitcast(I32))
        w4_s = reused.tile([P, R_BLOCKS, N], U8, name="w4_s", align_bytes=64, offset=R_BLOCKS * 2 * N)
        nc.vector.memset(w4_s[:].bitcast(I32), 0)
        for q in range(P // QUADRANT):
            nc.sync.dma_start(
                w4_s[QUADRANT * q : QUADRANT * q + PACK].bitcast(I32),
                w4_scales[:, PACK * q : PACK * (q + 1), :].rearrange("b r c -> r b c").bitcast(I32),
            )

        pairs = [(b, a, u) for b in range(1, R_BLOCKS) for u in range(2) for a in range(K_PASSES)]

        ADD_LAG, QUANT_LAG = 2, 3
        lagged = [k for k in range(1, last - 2, 2)]

        products(0)
        copy_factory(0)
        products(1)
        for k in range(len(steps)):
            ahead = k + 2
            weights_ready = ahead <= last and all((steps[ahead][0], a, t // 2) in w1_c for a in range(K_PASSES) for t in steps[ahead][3])
            if k < last:
                copy_factory(k + 1)
            differences(k)
            if weights_ready:
                products(ahead)
            magnitudes(k)
            for n, pair in enumerate(pairs):
                if (n + 1) // 2 == k:
                    round_w1(*pair, n % 2 == 0)
            if k - ADD_LAG in lagged:
                add_h(k - ADD_LAG)
            for n, pair in enumerate(pairs):
                if (n + 1) // 2 == k - 1:
                    quantise_w1(*pair)
            if ahead <= last and not weights_ready:
                products(ahead)
            if k - QUANT_LAG in lagged:
                quantise_h(k - QUANT_LAG)
                done_b, done_j0 = steps[k - QUANT_LAG][:2]
                if done_j0 == 0:
                    for o in FIRST_HALF:
                        scores(o, done_b)
            if k == last - 1:
                add_h(last - 2)
                for o in SECOND_HALF:
                    scores(o, 0)
                store(0, False)
        quantise_h(last - 2)
        add_h(last - 1)
        for o in SECOND_HALF:
            scores(o, 1)
        quantise_h(last - 1)
        add_h(last)
        scores(2, R_BLOCKS - 1)
        store(1, False)
        quantise_h(last)
        scores(3, R_BLOCKS - 1)
        scores(4, R_BLOCKS - 1)
        store(2, False)
        store(3, False)
        store(4, True)
